import numpy as np
import ml_dtypes


def mxq(x, axis, fmt="e4m3"):
    dtype, down = {"e4m3": (ml_dtypes.float8_e4m3fn, 7), "e5m2": (ml_dtypes.float8_e5m2, 14)}[fmt]
    v = np.moveaxis(np.asarray(x, np.float32).astype(ml_dtypes.bfloat16).astype(np.float64), axis, -1)
    blocks = v.reshape(v.shape[:-1] + (-1, 32))
    amax = np.abs(blocks).max(-1, keepdims=True)
    byte = np.maximum(np.where(amax > 0, np.frexp(amax)[1] - 1 + 127, 0) - down, 1)
    scale = np.exp2(byte - 127.0)
    codes = (blocks / scale).astype(np.float32).astype(dtype).astype(np.float64)
    return np.moveaxis((codes * scale).reshape(v.shape), -1, axis)


WIDE = False


def mx_kscale(k):
    if not WIDE:
        return np.ones(k)
    levels = np.array([10, -10, 5, -5, 0])
    if k % 512:
        return np.exp2(np.random.permutation(np.resize(levels, k // 32))).repeat(32)
    a = np.empty((k // 512, 16))
    for p in range(k // 512):
        a[p, :8] = np.random.permutation(np.resize(levels, 8))
        for g in range(8):
            far = levels[np.abs(levels - a[p, g]) >= 10]
            a[p, g + 8] = far[np.random.randint(len(far))]
    return np.exp2(a.ravel()).repeat(32)


BF16 = ml_dtypes.bfloat16


def bf(x):
    return np.asarray(x, np.float32).astype(BF16)


def f64(x):
    return np.asarray(x).astype(np.float64)


E2M1 = np.array([0.0, 0.5, 1.0, 1.5, 2.0, 3.0, 4.0, 6.0, -0.0, -0.5, -1.0, -1.5, -2.0, -3.0, -4.0, -6.0])


def pack_weight(w, fmt):
    k, n = w.shape
    w = f64(bf(w)).reshape(k // 32, 32, n)
    amax = np.abs(w).max(1)
    if fmt == "e4m3":
        byte = np.frexp(amax)[1] - 1 + 127 - 7
    else:
        mant, ex = np.frexp(amax / 6.0)
        byte = np.where(mant > 0.5, ex, ex - 1) + 127
    byte = np.clip(np.where(amax > 0, byte, 1), 1, 254)
    scaled = (w * np.exp2(127.0 - byte)[:, None, :]).reshape(k, n).astype(np.float32)
    by_word = np.ascontiguousarray(scaled.reshape(k // 512, 128, 4, n).transpose(0, 1, 3, 2))
    if fmt == "e4m3":
        words = by_word.astype(ml_dtypes.float8_e4m3fn).view(np.uint8)
    else:
        c = by_word.astype(ml_dtypes.float4_e2m1fn).view(np.uint8) & 0xF
        words = c[..., 0::2] | (c[..., 1::2] << 4)
    return np.ascontiguousarray(words), np.ascontiguousarray(byte.astype(np.uint8).reshape(k // 512, 16, n))


def unpack_weight(words, scales, fmt):
    g, p, n, _ = words.shape
    if fmt == "e4m3":
        vals = np.ascontiguousarray(words).view(ml_dtypes.float8_e4m3fn).astype(np.float64)
    else:
        nib = np.empty((g, p, n, 4), np.uint8)
        nib[..., 0::2] = words & 0xF
        nib[..., 1::2] = words >> 4
        vals = E2M1[nib]
    vals = vals * np.repeat(np.exp2(scales.astype(np.float64) - 127.0), 8, axis=1)[..., None]
    return vals.transpose(0, 1, 3, 2).reshape(g * 512, n)
def pack4(w):
    words, scales = pack_weight(w, "e2m1")
    return words.reshape(words.shape[0], 128, -1), scales


def unpack4(words, scales):
    return unpack_weight(words.reshape(words.shape[0], 128, -1, 2), scales, "e2m1")


G, M, N, F, R = 4, 1024, 1024, 512, 512


def setup_inputs():
    s = mx_kscale(G * N)
    t = mx_kscale(G * F)
    impact = np.random.standard_normal((G * N, F)) / np.sqrt(N) / s[:, None]
    contrast = np.random.standard_normal((G * F, R)) / np.sqrt(F) / t[:, None]
    b_words, b_scales = pack4(impact)
    c_words, c_scales = pack4(contrast)
    return {"psi": bf(np.random.standard_normal((G, M, N)) * s.reshape(G, 1, N)),
            "b_words": b_words,
            "b_scales": b_scales,
            "shock_var": bf(np.exp(0.3 * np.random.standard_normal((G, F))) * t.reshape(G, F)),
            "c_words": c_words,
            "c_scales": c_scales,
            "total_var": bf(np.exp(0.3 * np.random.standard_normal((G, M))))}


def reference(psi, b_words, b_scales, shock_var, c_words, c_scales, total_var):
    b = unpack4(b_words, b_scales).reshape(G, N, F)
    c = unpack4(c_words, c_scales).reshape(G, F, R)
    theta = mxq(f64(psi), 2, "e4m3") @ b
    v = theta ** 2 * f64(shock_var)[:, None, :]
    y = mxq(v, 2, "e4m3") @ c
    return y / f64(total_var)[:, :, None]

@@ -1,0 +1,287 @@
+from contextlib import ExitStack
+
+import concourse.mybir as mybir
+from concourse.masks import make_identity
+
+G, M, N, F, R = 4, 1024, 1024, 512, 512
+FLOPS = 2 * G * M * (N * F + F * R)
+
+F32 = mybir.dt.float32
+BF16 = mybir.dt.bfloat16
+I32 = mybir.dt.int32
+U32 = mybir.dt.uint32
+U8 = mybir.dt.uint8
+FP8X4 = mybir.dt.float8_e4m3fn_x4
+FP4X4 = mybir.dt.float4_e2m1fn_x4
+ACT = mybir.ActivationFunctionType
+ALU = mybir.AluOpType
+
+P = 128
+PACK = 4
+K_PASS = P * PACK
+PASSES = N // K_PASS
+ROWS = M // P
+UNIT = 4
+UNITS = G * ROWS // UNIT
+TILES = G * ROWS
+AHEAD = 6
+BANKS = 8
+
+
+def tile_svar_horizon_variance_contrasts_s14_kernel(
+    tc, psi, b_words, b_scales, shock_var, c_words, c_scales, total_var, out
+):
+    nc = tc.nc
+    with ExitStack() as ctx:
+        keep = ctx.enter_context(tc.tile_pool(name="keep", bufs=1))
+        work = ctx.enter_context(tc.tile_pool(name="work", bufs=2))
+        outs = ctx.enter_context(tc.tile_pool(name="outs", bufs=6))
+        psum = ctx.enter_context(tc.psum_pool(name="psum", bufs=1))
+        ctx.enter_context(tc.manual_schedule())
+
+        bank_uses = []
+
+        def take_bank():
+            name = "bank%d" % (len(bank_uses) % BANKS)
+            bank = psum.tile([P, K_PASS], F32, name=name, tag=name)
+            bank_uses.append(name)
+            return bank
+
+        ident = keep.tile([P, P], F32, align_bytes=64)
+        make_identity(nc, ident[:])
+
+        bs_first = keep.tile([P, PASSES * F], U8, align_bytes=64)
+        bs_rest = keep.tile([P, (G - 1) * PASSES * F], U8, align_bytes=64)
+        cs = keep.tile([P, G * R], U8, align_bytes=64)
+        nc.vector.memset(bs_first[:].bitcast(I32), 0)
+        nc.vector.memset(cs[:].bitcast(I32), 0)
+        nc.vector.memset(bs_rest[:].bitcast(I32), 0)
+
+        def load_scale_rows(plane, rows):
+            for q in range(4):
+                nc.sync.dma_start(
+                    out=plane[32 * q : 32 * q + 4, :].bitcast(I32).rearrange("p (g w) -> p g w", g=rows.shape[0]),
+                    in_=rows[:, 4 * q : 4 * q + 4, :].bitcast(I32).rearrange("g r w -> r g w"),
+                )
+
+        psi_pairs = []
+
+        def load_psi_pair():
+            n = len(psi_pairs)
+            a, j = divmod(2 * n, ROWS)
+            pair = keep.tile([P, 2, N], BF16, name="psi%d" % n, align_bytes=64)
+            nc.sync.dma_start(out=pair[:], in_=psi[a].rearrange("(p j) k -> p j k", j=ROWS)[:, j : j + 2, :])
+            psi_pairs.append(pair)
+
+        b_raw = []
+
+        def load_b_words():
+            a = len(b_raw)
+            raw = keep.tile([P, PASSES * 2 * F], U8, name="braw%d" % a, align_bytes=64)
+            nc.sync.dma_start(
+                out=raw[:].bitcast(I32).rearrange("p (g w) -> p g w", g=PASSES),
+                in_=b_words[PASSES * a : PASSES * (a + 1)].bitcast(I32).rearrange("g p w -> p g w"),
+            )
+            b_raw.append(raw)
+
+        sv = keep.tile([P, G, PACK], BF16, align_bytes=64)
+        tv = keep.tile([P, G, ROWS], BF16, align_bytes=64)
+        cw = keep.tile([P, G * 2 * R], U8, align_bytes=64)
+
+        nc.scalar.dma_start(out=sv[:], in_=shock_var.rearrange("a (p t) -> p a t", t=PACK))
+        load_psi_pair()
+        load_b_words()
+        load_scale_rows(bs_first, b_scales[0:PASSES])
+        load_psi_pair()
+        load_psi_pair()
+        load_psi_pair()
+        nc.sync.dma_start(out=tv[:], in_=total_var.rearrange("a (p j) -> p a j", j=ROWS))
+        load_b_words()
+        load_scale_rows(bs_rest, b_scales[PASSES:])
+        load_scale_rows(cs, c_scales)
+        load_psi_pair()
+        nc.sync.dma_start(
+            out=cw[:].bitcast(I32).rearrange("p (g w) -> p g w", g=G),
+            in_=c_words.bitcast(I32).rearrange("g p w -> p g w"),
+        )
+        for n in range(3):
+            load_psi_pair()
+        load_b_words()
+        for n in range(4):
+            load_psi_pair()
+        load_b_words()
+        for n in range(4):
+            load_psi_pair()
+
+        s0 = keep.tile([P, G * PACK], F32)
+        sv_flat = sv[:].rearrange("p a t -> p (a t)")
+        nc.scalar.activation(out=s0[:], in_=sv_flat, func=ACT.Sqrt)
+
+        b_codes = []
+        b_planes = []
+        for a in range(G):
+            codes = keep.tile([P, PACK, PASSES * 2 * P], U8, name="bcodes%d" % a, align_bytes=64)
+            plane = keep.tile([P, PACK, PASSES * P], U8, name="bplane%d" % a, align_bytes=64)
+            b_codes.append(codes)
+            b_planes.append(plane)
+
+        def sort_b(a, t0, t1):
+            nc.vector.tensor_copy(
+                out=b_codes[a][:, t0:t1, :].rearrange("p t (m b) -> p t m b", b=2),
+                in_=b_raw[a][:].rearrange("p (m t b) -> p t m b", t=PACK, b=2)[:, t0:t1, :, :],
+            )
+            width = PASSES * F
+            raw = bs_first[:] if a == 0 else bs_rest[:, (a - 1) * width : a * width]
+            nc.vector.tensor_copy(
+                out=b_planes[a][:, t0:t1, :],
+                in_=raw.rearrange("p (m t) -> p t m", t=PACK)[:, t0:t1, :],
+            )
+
+        x_words = {}
+
+        def transpose_tile(n):
+            u, j = divmod(n, UNIT)
+            if j == 0:
+                x_words[u] = work.tile([P, PASSES, UNIT, P, 2], F32, name="xw", tag="xw", align_bytes=64)
+            words = psi_pairs[n // 2][:, n % 2, :].bitcast(F32)
+            bank = take_bank()
+            for g in range(PASSES):
+                for h in range(2):
+                    c = (2 * g + h) * P
+                    nc.tensor.transpose(bank[:, c : c + P], words[:, 2 * P * g + h : 2 * P * (g + 1) : 2], ident[:])
+            return bank
+
+        def copy_tile(n, bank, on_scalar):
+            u, j = divmod(n, UNIT)
+            dst = x_words[u][:, :, j, :, :]
+            src = bank[:].rearrange("p (g h r) -> p g r h", g=PASSES, h=2)
+            if on_scalar:
+                nc.scalar.copy(out=dst, in_=src)
+            else:
+                nc.vector.tensor_copy(out=dst, in_=src)
+
+        x_q = {}
+
+        def quantize_x(u):
+            codes = work.tile([P, PASSES, K_PASS], U32, name="xc", tag="xc", align_bytes=64)
+            plane = work.tile([P, PASSES, K_PASS], U8, name="xs", tag="xs", align_bytes=64)
+            for g in range(PASSES):
+                nc.vector.quantize_mx(
+                    out=codes[:, g, :].bitcast(FP8X4),
+                    scales=plane[:, g, :],
+                    in_=x_words[u][:, g, :, :, :].rearrange("p j r h -> p (j r h)").bitcast(BF16),
+                )
+            x_q[u] = (codes, plane)
+
+        root = keep.tile([P, G * PACK], F32)
+        inv_tv = keep.tile([P, G * ROWS], F32)
+
+        def polish_root():
+            guard = keep.tile([P, G * PACK], F32)
+            inv = keep.tile([P, G * PACK], F32)
+            half = keep.tile([P, G * PACK], F32)
+            nc.vector.tensor_scalar(out=guard[:], in0=s0[:], scalar1=1e-30, scalar2=None, op0=ALU.max)
+            nc.vector.reciprocal(out=inv[:], in_=guard[:])
+            nc.vector.scalar_tensor_tensor(
+                out=half[:], in0=sv_flat, scalar=0.5, in1=inv[:], op0=ALU.mult, op1=ALU.mult
+            )
+            nc.vector.scalar_tensor_tensor(
+                out=root[:], in0=s0[:], scalar=0.5, in1=half[:], op0=ALU.mult, op1=ALU.add
+            )
+
+        def stage_one(u):
+            a = u // 2
+            codes, plane = x_q[u]
+            v_rows = work.tile([P, PACK, K_PASS], BF16, name="vrows", tag="vrows", align_bytes=64)
+            for t in range(PACK):
+                bank = take_bank()
+                for g in range(PASSES):
+                    nc.tensor.matmul_mx(
+                        out=bank[:],
+                        lhsT=b_codes[a][:, t, 2 * P * g : 2 * P * (g + 1)].bitcast(FP4X4),
+                        lhsT_scale=b_planes[a][:, t, P * g : P * (g + 1)],
+                        rhs=codes[:, g, :].bitcast(FP8X4),
+                        rhs_scale=plane[:, g, :],
+                        start=(g == 0),
+                        stop=(g == PASSES - 1),
+                    )
+                c = PACK * a + t
+                nc.scalar.activation(out=v_rows[:, t, :], in_=bank[:], func=ACT.Square, scale=root[:, c : c + 1])
+            return v_rows
+
+        def interleave_v(v_rows):
+            v_words = work.tile([P, K_PASS, PACK], BF16, name="vwords", tag="vwords", align_bytes=64)
+            nc.vector.tensor_copy(
+                out=v_words[:].rearrange("p (c i) t -> p c t i", i=4),
+                in_=v_rows[:].rearrange("p t (c i) -> p c t i", i=4),
+            )
+            return v_words
+
+        v_q = {}
+
+        def quantize_v(u, v_words):
+            codes = work.tile([P, K_PASS], U32, name="vc", tag="vc", align_bytes=64)
+            plane = work.tile([P, K_PASS], U8, name="vs", tag="vs", align_bytes=64)
+            nc.vector.quantize_mx(
+                out=codes[:].bitcast(FP8X4), scales=plane[:], in_=v_words[:].rearrange("p c t -> p (c t)")
+            )
+            v_q[u] = (codes, plane)
+
+        def stage_two(u, on_scalar, split_store):
+            a, h = divmod(u, 2)
+            codes, plane = v_q[u]
+            result = outs.tile([P, UNIT, R], F32, name="result", tag="result")
+            dst = out[a].rearrange("(p j) r -> p j r", j=ROWS)
+            for j in range(UNIT):
+                bank = take_bank()
+                nc.tensor.matmul_mx(
+                    out=bank[:],
+                    lhsT=codes[:, P * j : P * (j + 1)].bitcast(FP8X4),
+                    lhsT_scale=plane[:, P * j : P * (j + 1)],
+                    rhs=cw[:, 2 * R * a : 2 * R * (a + 1)].bitcast(FP4X4),
+                    rhs_scale=cs[:, R * a : R * (a + 1)],
+                    start=True,
+                    stop=True,
+                )
+                c = ROWS * a + UNIT * h + j
+                if j in on_scalar:
+                    nc.scalar.activation(out=result[:, j, :], in_=bank[:], func=ACT.Copy, scale=inv_tv[:, c : c + 1])
+                else:
+                    nc.vector.tensor_scalar(
+                        out=result[:, j, :], in0=bank[:], scalar1=inv_tv[:, c : c + 1], scalar2=None, op0=ALU.mult
+                    )
+                if split_store:
+                    nc.sync.dma_start(out=dst[:, UNIT * h + j, :], in_=result[:, j, :])
+            if not split_store:
+                nc.sync.dma_start(out=dst[:, UNIT * h : UNIT * (h + 1), :], in_=result[:])
+
+        sort_b(0, 0, PACK)
+        polish_root()
+        for n in range(AHEAD):
+            bank = transpose_tile(n)
+            copy_tile(n, bank, True)
+            if n == UNIT - 1:
+                quantize_x(0)
+        nc.vector.reciprocal(out=inv_tv[:], in_=tv[:].rearrange("p a j -> p (a j)"))
+
+        for u in range(UNITS):
+            v_rows = stage_one(u)
+            late = None
+            for n in range(UNIT * u + AHEAD, min(UNIT * (u + 1) + AHEAD, TILES)):
+                bank = transpose_tile(n)
+                if n % UNIT == 1:
+                    late = (n, bank)
+                else:
+                    copy_tile(n, bank, True)
+            v_words = interleave_v(v_rows)
+            if u + 1 < UNITS:
+                quantize_x(u + 1)
+            quantize_v(u, v_words)
+            if late is not None:
+                copy_tile(late[0], late[1], False)
+            if u > 0:
+                stage_two(u - 1, (0, 1), False)
+            a, h = divmod(u, 2)
+            if a + 1 < G:
+                sort_b(a + 1, 2 * h, 2 * h + 2)
+        stage_two(UNITS - 1, (0, 2), True)

@@ -64,14 +64,15 @@ def tile_svar_horizon_variance_contrasts_s14_kernel(
                     in_=rows[:, 4 * q : 4 * q + 4, :].bitcast(I32).rearrange("g r w -> r g w"),
                 )
 
-        psi_pairs = []
+        psi_tiles = []
 
-        def load_psi_pair():
-            n = len(psi_pairs)
-            a, j = divmod(2 * n, ROWS)
-            pair = keep.tile([P, 2, N], BF16, name="psi%d" % n, align_bytes=64)
-            nc.sync.dma_start(out=pair[:], in_=psi[a].rearrange("(p j) k -> p j k", j=ROWS)[:, j : j + 2, :])
-            psi_pairs.append(pair)
+        def load_psi(count):
+            n = len(psi_tiles)
+            a, j = divmod(n, ROWS)
+            rows = keep.tile([P, count, N], BF16, name="psi%d" % n, align_bytes=64)
+            nc.sync.dma_start(out=rows[:], in_=psi[a].rearrange("(p j) k -> p j k", j=ROWS)[:, j : j + count, :])
+            for i in range(count):
+                psi_tiles.append(rows[:, i, :])
 
         b_raw = []
 
@@ -89,29 +90,30 @@ def tile_svar_horizon_variance_contrasts_s14_kernel(
         cw = keep.tile([P, G * 2 * R], U8, align_bytes=64)
 
         nc.scalar.dma_start(out=sv[:], in_=shock_var.rearrange("a (p t) -> p a t", t=PACK))
-        load_psi_pair()
+        load_psi(1)
+        load_psi(1)
+        load_psi(2)
         load_b_words()
         load_scale_rows(bs_first, b_scales[0:PASSES])
-        load_psi_pair()
-        load_psi_pair()
-        load_psi_pair()
+        load_psi(2)
+        load_psi(2)
         nc.sync.dma_start(out=tv[:], in_=total_var.rearrange("a (p j) -> p a j", j=ROWS))
+        load_psi(2)
         load_b_words()
         load_scale_rows(bs_rest, b_scales[PASSES:])
-        load_scale_rows(cs, c_scales)
-        load_psi_pair()
+        load_psi(2)
         nc.sync.dma_start(
             out=cw[:].bitcast(I32).rearrange("p (g w) -> p g w", g=G),
             in_=c_words.bitcast(I32).rearrange("g p w -> p g w"),
         )
-        for n in range(3):
-            load_psi_pair()
+        load_scale_rows(cs, c_scales)
+        load_psi(4)
         load_b_words()
-        for n in range(4):
-            load_psi_pair()
+        load_psi(4)
+        load_psi(4)
         load_b_words()
-        for n in range(4):
-            load_psi_pair()
+        load_psi(4)
+        load_psi(4)
 
         s0 = keep.tile([P, G * PACK], F32)
         sv_flat = sv[:].rearrange("p a t -> p (a t)")
@@ -138,40 +140,34 @@ def tile_svar_horizon_variance_contrasts_s14_kernel(
             )
 
         x_words = {}
+        x_q = {}
 
-        def transpose_tile(n):
+        def transpose_pair(n, g, on_scalar):
             u, j = divmod(n, UNIT)
             if j == 0:
-                x_words[u] = work.tile([P, PASSES, UNIT, P, 2], F32, name="xw", tag="xw", align_bytes=64)
-            words = psi_pairs[n // 2][:, n % 2, :].bitcast(F32)
+                x_words[u, g] = work.tile([P, UNIT, P, 2], F32, name="xw%d" % g, tag="xw%d" % g, align_bytes=64)
             bank = take_bank()
-            for g in range(PASSES):
+            for i in range(2):
+                words = psi_tiles[n + i].bitcast(F32)
                 for h in range(2):
-                    c = (2 * g + h) * P
+                    c = (2 * i + h) * P
                     nc.tensor.transpose(bank[:, c : c + P], words[:, 2 * P * g + h : 2 * P * (g + 1) : 2], ident[:])
-            return bank
-
-        def copy_tile(n, bank, on_scalar):
-            u, j = divmod(n, UNIT)
-            dst = x_words[u][:, :, j, :, :]
-            src = bank[:].rearrange("p (g h r) -> p g r h", g=PASSES, h=2)
+            dst = x_words[u, g][:, j : j + 2, :, :]
+            src = bank[:].rearrange("p (i h r) -> p i r h", i=2, h=2)
             if on_scalar:
                 nc.scalar.copy(out=dst, in_=src)
             else:
                 nc.vector.tensor_copy(out=dst, in_=src)
 
-        x_q = {}
-
-        def quantize_x(u):
-            codes = work.tile([P, PASSES, K_PASS], U32, name="xc", tag="xc", align_bytes=64)
-            plane = work.tile([P, PASSES, K_PASS], U8, name="xs", tag="xs", align_bytes=64)
-            for g in range(PASSES):
-                nc.vector.quantize_mx(
-                    out=codes[:, g, :].bitcast(FP8X4),
-                    scales=plane[:, g, :],
-                    in_=x_words[u][:, g, :, :, :].rearrange("p j r h -> p (j r h)").bitcast(BF16),
-                )
-            x_q[u] = (codes, plane)
+        def quantize_x(u, g):
+            codes = work.tile([P, K_PASS], U32, name="xc%d" % g, tag="xc%d" % g, align_bytes=64)
+            plane = work.tile([P, K_PASS], U8, name="xs%d" % g, tag="xs%d" % g, align_bytes=64)
+            nc.vector.quantize_mx(
+                out=codes[:].bitcast(FP8X4),
+                scales=plane[:],
+                in_=x_words[u, g][:].rearrange("p j r h -> p (j r h)").bitcast(BF16),
+            )
+            x_q[u, g] = (codes, plane)
 
         root = keep.tile([P, G * PACK], F32)
         inv_tv = keep.tile([P, G * ROWS], F32)
@@ -189,99 +185,141 @@ def tile_svar_horizon_variance_contrasts_s14_kernel(
                 out=root[:], in0=s0[:], scalar=0.5, in1=half[:], op0=ALU.mult, op1=ALU.add
             )
 
-        def stage_one(u):
-            a = u // 2
-            codes, plane = x_q[u]
-            v_rows = work.tile([P, PACK, K_PASS], BF16, name="vrows", tag="vrows", align_bytes=64)
-            for t in range(PACK):
-                bank = take_bank()
-                for g in range(PASSES):
-                    nc.tensor.matmul_mx(
-                        out=bank[:],
-                        lhsT=b_codes[a][:, t, 2 * P * g : 2 * P * (g + 1)].bitcast(FP4X4),
-                        lhsT_scale=b_planes[a][:, t, P * g : P * (g + 1)],
-                        rhs=codes[:, g, :].bitcast(FP8X4),
-                        rhs_scale=plane[:, g, :],
-                        start=(g == 0),
-                        stop=(g == PASSES - 1),
-                    )
-                c = PACK * a + t
-                nc.scalar.activation(out=v_rows[:, t, :], in_=bank[:], func=ACT.Square, scale=root[:, c : c + 1])
-            return v_rows
+        v_rows = {}
 
-        def interleave_v(v_rows):
-            v_words = work.tile([P, K_PASS, PACK], BF16, name="vwords", tag="vwords", align_bytes=64)
-            nc.vector.tensor_copy(
-                out=v_words[:].rearrange("p (c i) t -> p c t i", i=4),
-                in_=v_rows[:].rearrange("p t (c i) -> p c t i", i=4),
-            )
-            return v_words
+        def stage_one(u, t):
+            a = u // 2
+            if t == 0:
+                v_rows[u] = work.tile([P, PACK, K_PASS], BF16, name="vrows", tag="vrows", align_bytes=64)
+            bank = take_bank()
+            for g in range(PASSES):
+                nc.tensor.matmul_mx(
+                    out=bank[:],
+                    lhsT=b_codes[a][:, t, 2 * P * g : 2 * P * (g + 1)].bitcast(FP4X4),
+                    lhsT_scale=b_planes[a][:, t, P * g : P * (g + 1)],
+                    rhs=x_q[u, g][0][:].bitcast(FP8X4),
+                    rhs_scale=x_q[u, g][1][:],
+                    start=(g == 0),
+                    stop=(g == PASSES - 1),
+                )
+            c = PACK * a + t
+            nc.scalar.activation(out=v_rows[u][:, t, :], in_=bank[:], func=ACT.Square, scale=root[:, c : c + 1])
 
         v_q = {}
 
-        def quantize_v(u, v_words):
+        def new_v(u):
+            v_words = work.tile([P, K_PASS, PACK], BF16, name="vwords", tag="vwords", align_bytes=64)
             codes = work.tile([P, K_PASS], U32, name="vc", tag="vc", align_bytes=64)
             plane = work.tile([P, K_PASS], U8, name="vs", tag="vs", align_bytes=64)
-            nc.vector.quantize_mx(
-                out=codes[:].bitcast(FP8X4), scales=plane[:], in_=v_words[:].rearrange("p c t -> p (c t)")
+            v_q[u] = (v_words, codes, plane)
+
+        def interleave_v(u, j0, j1):
+            nc.vector.tensor_copy(
+                out=v_q[u][0][:, P * j0 : P * j1, :].rearrange("p (c i) t -> p c t i", i=4),
+                in_=v_rows[u][:, :, P * j0 : P * j1].rearrange("p t (c i) -> p c t i", i=4),
             )
-            v_q[u] = (codes, plane)
 
-        def stage_two(u, on_scalar, split_store):
-            a, h = divmod(u, 2)
-            codes, plane = v_q[u]
-            result = outs.tile([P, UNIT, R], F32, name="result", tag="result")
-            dst = out[a].rearrange("(p j) r -> p j r", j=ROWS)
-            for j in range(UNIT):
-                bank = take_bank()
-                nc.tensor.matmul_mx(
-                    out=bank[:],
-                    lhsT=codes[:, P * j : P * (j + 1)].bitcast(FP8X4),
-                    lhsT_scale=plane[:, P * j : P * (j + 1)],
-                    rhs=cw[:, 2 * R * a : 2 * R * (a + 1)].bitcast(FP4X4),
-                    rhs_scale=cs[:, R * a : R * (a + 1)],
-                    start=True,
-                    stop=True,
+        def quantize_v(u, j0, j1):
+            v_words, codes, plane = v_q[u]
+            nc.vector.quantize_mx(
+                out=codes[:, P * j0 : P * j1].bitcast(FP8X4),
+                scales=plane[:, P * j0 : P * j1],
+                in_=v_words[:, P * j0 : P * j1, :].rearrange("p c t -> p (c t)"),
+            )
+
+        results = {}
+
+        def stage_two(u, j):
+            a = u // 2
+            v_words, codes, plane = v_q[u]
+            bank = take_bank()
+            nc.tensor.matmul_mx(
+                out=bank[:],
+                lhsT=codes[:, P * j : P * (j + 1)].bitcast(FP8X4),
+                lhsT_scale=plane[:, P * j : P * (j + 1)],
+                rhs=cw[:, 2 * R * a : 2 * R * (a + 1)].bitcast(FP4X4),
+                rhs_scale=cs[:, R * a : R * (a + 1)],
+                start=True,
+                stop=True,
+            )
+            return bank
+
+        def finish(u, j, bank, on_scalar):
+            if j == 0:
+                results[u] = outs.tile([P, UNIT, R], F32, name="result", tag="result")
+            c = UNIT * u + j
+            if on_scalar:
+                nc.scalar.activation(out=results[u][:, j, :], in_=bank[:], func=ACT.Copy, scale=inv_tv[:, c : c + 1])
+            else:
+                nc.vector.tensor_scalar(
+                    out=results[u][:, j, :], in0=bank[:], scalar1=inv_tv[:, c : c + 1], scalar2=None, op0=ALU.mult
                 )
-                c = ROWS * a + UNIT * h + j
-                if j in on_scalar:
-                    nc.scalar.activation(out=result[:, j, :], in_=bank[:], func=ACT.Copy, scale=inv_tv[:, c : c + 1])
-                else:
-                    nc.vector.tensor_scalar(
-                        out=result[:, j, :], in0=bank[:], scalar1=inv_tv[:, c : c + 1], scalar2=None, op0=ALU.mult
-                    )
-                if split_store:
-                    nc.sync.dma_start(out=dst[:, UNIT * h + j, :], in_=result[:, j, :])
-            if not split_store:
-                nc.sync.dma_start(out=dst[:, UNIT * h : UNIT * (h + 1), :], in_=result[:])
 
-        sort_b(0, 0, PACK)
-        polish_root()
-        for n in range(AHEAD):
-            bank = transpose_tile(n)
-            copy_tile(n, bank, True)
-            if n == UNIT - 1:
-                quantize_x(0)
-        nc.vector.reciprocal(out=inv_tv[:], in_=tv[:].rearrange("p a j -> p (a j)"))
-
-        for u in range(UNITS):
-            v_rows = stage_one(u)
-            late = None
-            for n in range(UNIT * u + AHEAD, min(UNIT * (u + 1) + AHEAD, TILES)):
-                bank = transpose_tile(n)
-                if n % UNIT == 1:
-                    late = (n, bank)
-                else:
-                    copy_tile(n, bank, True)
-            v_words = interleave_v(v_rows)
-            if u + 1 < UNITS:
-                quantize_x(u + 1)
-            quantize_v(u, v_words)
-            if late is not None:
-                copy_tile(late[0], late[1], False)
-            if u > 0:
-                stage_two(u - 1, (0, 1), False)
+        def store(u, j0, j1):
             a, h = divmod(u, 2)
-            if a + 1 < G:
+            dst = out[a].rearrange("(p j) r -> p j r", j=ROWS)
+            nc.sync.dma_start(out=dst[:, UNIT * h + j0 : UNIT * h + j1, :], in_=results[u][:, j0:j1, :])
+
+        def pair(n, first, second):
+            transpose_pair(n, 0, first)
+            transpose_pair(n, 1, second)
+
+        polish_root()
+        pair(0, True, True)
+        sort_b(0, 0, 2)
+        transpose_pair(2, 0, True)
+        quantize_x(0, 0)
+        transpose_pair(2, 1, True)
+        quantize_x(0, 1)
+        sort_b(0, 2, 4)
+        pair(4, True, True)
+
+        last = UNITS - 1
+        for u in range(UNITS):
+            n = UNIT * u + AHEAD
+            early = u in (0, last - 1)
+            for t in range(PACK):
+                stage_one(u, t)
+                if early and t == 1:
+                    pair(n, False, False)
+                    quantize_x(u + 1, 0)
+                    quantize_x(u + 1, 1)
+            if u == 0:
+                pair(n + 2, True, True)
+                nc.vector.reciprocal(out=inv_tv[:], in_=tv[:].rearrange("p a j -> p (a j)"))
+            elif n < TILES and not early:
+                pair(n, True, True)
+            new_v(u)
+            if u < last:
+                interleave_v(u, 0, UNIT)
+                if not early:
+                    quantize_x(u + 1, 0)
+                    quantize_x(u + 1, 1)
+                if u == 0:
+                    sort_b(1, 0, 2)
+                if u != last - 1:
+                    quantize_v(u, 0, UNIT)
+            a, h = divmod(u + 1, 2)
+            sorting = a + 1 < G
+            if u > 0:
+                for j in range(UNIT):
+                    finish(u - 1, j, stage_two(u - 1, j), j < 2 or u == last)
+                    if u == last - 1 and j == 2:
+                        quantize_v(u, 0, UNIT)
+                    if u == last:
+                        store(u - 1, j, j + 1)
+                    elif j % 2 == 1:
+                        store(u - 1, j - 1, j + 1)
+            if u > 0 and n + 2 < TILES:
+                pair(n + 2, True, sorting)
+            if sorting:
                 sort_b(a + 1, 2 * h, 2 * h + 2)
-        stage_two(UNITS - 1, (0, 2), True)
+        u = last
+        interleave_v(u, 0, 1)
+        for j in range(UNIT):
+            if j + 1 < UNIT:
+                interleave_v(u, j + 1, j + 2)
+            quantize_v(u, j, j + 1)
+        for j in range(UNIT):
+            finish(u, j, stage_two(u, j), j % 2 == 1)
+            store(u, j, j + 1)

@@ -17,15 +17,20 @@ ACT = mybir.ActivationFunctionType
 ALU = mybir.AluOpType
 
 P = 128
-PACK = 4
-K_PASS = P * PACK
+SLOTS = 4
+K_PASS = P * SLOTS
 PASSES = N // K_PASS
-ROWS = M // P
-UNIT = 4
-UNITS = G * ROWS // UNIT
-TILES = G * ROWS
-AHEAD = 6
+FP4_BYTES = 2
+QUADRANT = 32
+TILES_PER_REGIME = M // P
+TILES_PER_UNIT = 4
+UNIT_ROWS = TILES_PER_UNIT * P
+UNITS_PER_REGIME = TILES_PER_REGIME // TILES_PER_UNIT
+UNITS = G * UNITS_PER_REGIME
+TILES = G * TILES_PER_REGIME
 BANKS = 8
+RESULT_BUFS = 6
+ON_SCALAR, ON_VECTOR = True, False
 
 
 def tile_svar_horizon_variance_contrasts_s14_kernel(
@@ -35,7 +40,7 @@ def tile_svar_horizon_variance_contrasts_s14_kernel(
     with ExitStack() as ctx:
         keep = ctx.enter_context(tc.tile_pool(name="keep", bufs=1))
         work = ctx.enter_context(tc.tile_pool(name="work", bufs=2))
-        outs = ctx.enter_context(tc.tile_pool(name="outs", bufs=6))
+        outs = ctx.enter_context(tc.tile_pool(name="outs", bufs=RESULT_BUFS))
         psum = ctx.enter_context(tc.psum_pool(name="psum", bufs=1))
         ctx.enter_context(tc.manual_schedule())
 
@@ -50,276 +55,287 @@ def tile_svar_horizon_variance_contrasts_s14_kernel(
         ident = keep.tile([P, P], F32, align_bytes=64)
         make_identity(nc, ident[:])
 
-        bs_first = keep.tile([P, PASSES * F], U8, align_bytes=64)
-        bs_rest = keep.tile([P, (G - 1) * PASSES * F], U8, align_bytes=64)
-        cs = keep.tile([P, G * R], U8, align_bytes=64)
-        nc.vector.memset(bs_first[:].bitcast(I32), 0)
-        nc.vector.memset(cs[:].bitcast(I32), 0)
-        nc.vector.memset(bs_rest[:].bitcast(I32), 0)
+        b_scale_first = keep.tile([P, PASSES * F], U8, align_bytes=64)
+        b_scale_rest = keep.tile([P, (G - 1) * PASSES * F], U8, align_bytes=64)
+        c_planes = keep.tile([P, G * R], U8, align_bytes=64)
+        nc.vector.memset(b_scale_first[:].bitcast(I32), 0)
+        nc.vector.memset(c_planes[:].bitcast(I32), 0)
+        nc.vector.memset(b_scale_rest[:].bitcast(I32), 0)
 
-        def load_scale_rows(plane, rows):
-            for q in range(4):
+
+        def load_scale_rows(planes, rows):
+            for q in range(P // QUADRANT):
                 nc.sync.dma_start(
-                    out=plane[32 * q : 32 * q + 4, :].bitcast(I32).rearrange("p (g w) -> p g w", g=rows.shape[0]),
+                    out=planes[QUADRANT * q : QUADRANT * q + 4, :]
+                    .bitcast(I32)
+                    .rearrange("p (g w) -> p g w", g=rows.shape[0]),
                     in_=rows[:, 4 * q : 4 * q + 4, :].bitcast(I32).rearrange("g r w -> r g w"),
                 )
 
-        psi_tiles = []
+        psi_words = {}
 
-        def load_psi(count):
-            n = len(psi_tiles)
-            a, j = divmod(n, ROWS)
+        def load_psi(n, count):
+            a, s = divmod(n, TILES_PER_REGIME)
             rows = keep.tile([P, count, N], BF16, name="psi%d" % n, align_bytes=64)
-            nc.sync.dma_start(out=rows[:], in_=psi[a].rearrange("(p j) k -> p j k", j=ROWS)[:, j : j + count, :])
-            for i in range(count):
-                psi_tiles.append(rows[:, i, :])
+            src = psi[a].rearrange("(p s) k -> p s k", s=TILES_PER_REGIME)
+            nc.sync.dma_start(out=rows[:], in_=src[:, s : s + count, :])
+            for i in range(0, count, 2):
+                for g in range(PASSES):
+                    psi_words[n + i, g] = rows[:, i : i + 2, g * K_PASS : (g + 1) * K_PASS].bitcast(F32)
 
-        b_raw = []
+        b_raw = {}
 
-        def load_b_words():
-            a = len(b_raw)
-            raw = keep.tile([P, PASSES * 2 * F], U8, name="braw%d" % a, align_bytes=64)
+        def load_b_words(a):
+            b_raw[a] = keep.tile([P, PASSES * FP4_BYTES * F], U8, name="braw%d" % a, align_bytes=64)
             nc.sync.dma_start(
-                out=raw[:].bitcast(I32).rearrange("p (g w) -> p g w", g=PASSES),
+                out=b_raw[a][:].bitcast(I32).rearrange("p (g w) -> p g w", g=PASSES),
                 in_=b_words[PASSES * a : PASSES * (a + 1)].bitcast(I32).rearrange("g p w -> p g w"),
             )
-            b_raw.append(raw)
 
-        sv = keep.tile([P, G, PACK], BF16, align_bytes=64)
-        tv = keep.tile([P, G, ROWS], BF16, align_bytes=64)
-        cw = keep.tile([P, G * 2 * R], U8, align_bytes=64)
+        shock = keep.tile([P, G, SLOTS], BF16, align_bytes=64)
+        total = keep.tile([P, G, TILES_PER_REGIME], BF16, align_bytes=64)
+        c_codes = keep.tile([P, G * FP4_BYTES * R], U8, align_bytes=64)
 
-        nc.scalar.dma_start(out=sv[:], in_=shock_var.rearrange("a (p t) -> p a t", t=PACK))
-        load_psi(1)
-        load_psi(1)
-        load_psi(2)
-        load_b_words()
-        load_scale_rows(bs_first, b_scales[0:PASSES])
-        load_psi(2)
-        load_psi(2)
-        nc.sync.dma_start(out=tv[:], in_=total_var.rearrange("a (p j) -> p a j", j=ROWS))
-        load_psi(2)
-        load_b_words()
-        load_scale_rows(bs_rest, b_scales[PASSES:])
-        load_psi(2)
+        nc.scalar.dma_start(out=shock[:], in_=shock_var.rearrange("a (p t) -> p a t", t=SLOTS))
+        load_psi(0, 2)
+        load_b_words(0)
+        load_scale_rows(b_scale_first, b_scales[0:PASSES])
+        load_psi(2, 2)
+        load_psi(4, 2)
+        load_b_words(1)
+        load_scale_rows(b_scale_rest, b_scales[PASSES:])
+        load_psi(6, 2)
+        load_b_words(2)
+        load_psi(8, 2)
+        load_psi(10, 2)
+        nc.sync.dma_start(out=total[:], in_=total_var.rearrange("a (p s) -> p a s", s=TILES_PER_REGIME))
         nc.sync.dma_start(
-            out=cw[:].bitcast(I32).rearrange("p (g w) -> p g w", g=G),
+            out=c_codes[:].bitcast(I32).rearrange("p (g w) -> p g w", g=G),
             in_=c_words.bitcast(I32).rearrange("g p w -> p g w"),
         )
-        load_scale_rows(cs, c_scales)
-        load_psi(4)
-        load_b_words()
-        load_psi(4)
-        load_psi(4)
-        load_b_words()
-        load_psi(4)
-        load_psi(4)
+        load_scale_rows(c_planes, c_scales)
+        load_psi(12, TILES_PER_UNIT)
+        load_b_words(3)
+        for n in range(16, TILES, TILES_PER_UNIT):
+            load_psi(n, TILES_PER_UNIT)
 
-        s0 = keep.tile([P, G * PACK], F32)
-        sv_flat = sv[:].rearrange("p a t -> p (a t)")
-        nc.scalar.activation(out=s0[:], in_=sv_flat, func=ACT.Sqrt)
 
-        b_codes = []
-        b_planes = []
-        for a in range(G):
-            codes = keep.tile([P, PACK, PASSES * 2 * P], U8, name="bcodes%d" % a, align_bytes=64)
-            plane = keep.tile([P, PACK, PASSES * P], U8, name="bplane%d" % a, align_bytes=64)
-            b_codes.append(codes)
-            b_planes.append(plane)
+        b_codes = {}
+        b_planes = {}
 
-        def sort_b(a, t0, t1):
+        def sort_b_codes(a):
+            b_codes[a] = keep.tile([P, SLOTS, PASSES * FP4_BYTES * P], U8, name="bcodes%d" % a, align_bytes=64)
             nc.vector.tensor_copy(
-                out=b_codes[a][:, t0:t1, :].rearrange("p t (m b) -> p t m b", b=2),
-                in_=b_raw[a][:].rearrange("p (m t b) -> p t m b", t=PACK, b=2)[:, t0:t1, :, :],
+                out=b_codes[a][:].rearrange("p t (m b) -> p t m b", b=FP4_BYTES),
+                in_=b_raw[a][:].rearrange("p (m t b) -> p t m b", t=SLOTS, b=FP4_BYTES),
             )
+
+        def sort_b_scales(a):
             width = PASSES * F
-            raw = bs_first[:] if a == 0 else bs_rest[:, (a - 1) * width : a * width]
-            nc.vector.tensor_copy(
-                out=b_planes[a][:, t0:t1, :],
-                in_=raw.rearrange("p (m t) -> p t m", t=PACK)[:, t0:t1, :],
-            )
+            raw = b_scale_first[:] if a == 0 else b_scale_rest[:, (a - 1) * width : a * width]
+            b_planes[a] = keep.tile([P, SLOTS, PASSES * P], U8, name="bplane%d" % a, align_bytes=64)
+            nc.vector.tensor_copy(out=b_planes[a][:], in_=raw.rearrange("p (m t) -> p t m", t=SLOTS))
+
 
         x_words = {}
-        x_q = {}
+        x_mx = {}
 
-        def transpose_pair(n, g, on_scalar):
-            u, j = divmod(n, UNIT)
-            if j == 0:
-                x_words[u, g] = work.tile([P, UNIT, P, 2], F32, name="xw%d" % g, tag="xw%d" % g, align_bytes=64)
+        def transpose_pass(n, g, on_scalar):
+            u, c = divmod(n, TILES_PER_UNIT)
+            if c == 0:
+                name = "xwords%d" % g
+                x_words[u, g] = work.tile([P, TILES_PER_UNIT, P, 2], F32, name=name, tag=name, align_bytes=64)
             bank = take_bank()
             for i in range(2):
-                words = psi_tiles[n + i].bitcast(F32)
-                for h in range(2):
-                    c = (2 * i + h) * P
-                    nc.tensor.transpose(bank[:, c : c + P], words[:, 2 * P * g + h : 2 * P * (g + 1) : 2], ident[:])
-            dst = x_words[u, g][:, j : j + 2, :, :]
-            src = bank[:].rearrange("p (i h r) -> p i r h", i=2, h=2)
+                for odd in range(2):
+                    col = (2 * i + odd) * P
+                    nc.tensor.transpose(bank[:, col : col + P], psi_words[n, g][:, i, odd : 2 * P : 2], ident[:])
+            dst = x_words[u, g][:, c : c + 2, :, :]
+            src = bank[:].rearrange("p (i o r) -> p i r o", i=2, o=2)
             if on_scalar:
                 nc.scalar.copy(out=dst, in_=src)
             else:
                 nc.vector.tensor_copy(out=dst, in_=src)
 
+        def transpose_pair(n, second_on_scalar):
+            transpose_pass(n, 0, ON_SCALAR)
+            transpose_pass(n, 1, second_on_scalar)
+
         def quantize_x(u, g):
-            codes = work.tile([P, K_PASS], U32, name="xc%d" % g, tag="xc%d" % g, align_bytes=64)
-            plane = work.tile([P, K_PASS], U8, name="xs%d" % g, tag="xs%d" % g, align_bytes=64)
+            codes = work.tile([P, UNIT_ROWS], U32, name="xcodes%d" % g, tag="xcodes%d" % g, align_bytes=64)
+            plane = work.tile([P, UNIT_ROWS], U8, name="xplane%d" % g, tag="xplane%d" % g, align_bytes=64)
             nc.vector.quantize_mx(
                 out=codes[:].bitcast(FP8X4),
                 scales=plane[:],
-                in_=x_words[u, g][:].rearrange("p j r h -> p (j r h)").bitcast(BF16),
+                in_=x_words[u, g][:].rearrange("p c r o -> p (c r o)").bitcast(BF16),
             )
-            x_q[u, g] = (codes, plane)
+            x_mx[u, g] = (codes, plane)
 
-        root = keep.tile([P, G * PACK], F32)
-        inv_tv = keep.tile([P, G * ROWS], F32)
 
-        def polish_root():
-            guard = keep.tile([P, G * PACK], F32)
-            inv = keep.tile([P, G * PACK], F32)
-            half = keep.tile([P, G * PACK], F32)
-            nc.vector.tensor_scalar(out=guard[:], in0=s0[:], scalar1=1e-30, scalar2=None, op0=ALU.max)
-            nc.vector.reciprocal(out=inv[:], in_=guard[:])
+        root = keep.tile([P, G * SLOTS], F32)
+        inv_total = keep.tile([P, TILES], F32)
+
+        def make_root():
+            shock_flat = shock[:].rearrange("p a t -> p (a t)")
+            guess = keep.tile([P, G * SLOTS], F32)
+            floored = keep.tile([P, G * SLOTS], F32)
+            inv_guess = keep.tile([P, G * SLOTS], F32)
+            half_quotient = keep.tile([P, G * SLOTS], F32)
+            nc.scalar.activation(out=guess[:], in_=shock_flat, func=ACT.Sqrt)
+            nc.vector.tensor_scalar(out=floored[:], in0=guess[:], scalar1=1e-30, scalar2=None, op0=ALU.max)
+            nc.vector.reciprocal(out=inv_guess[:], in_=floored[:])
             nc.vector.scalar_tensor_tensor(
-                out=half[:], in0=sv_flat, scalar=0.5, in1=inv[:], op0=ALU.mult, op1=ALU.mult
+                out=half_quotient[:], in0=shock_flat, scalar=0.5, in1=inv_guess[:], op0=ALU.mult, op1=ALU.mult
             )
             nc.vector.scalar_tensor_tensor(
-                out=root[:], in0=s0[:], scalar=0.5, in1=half[:], op0=ALU.mult, op1=ALU.add
+                out=root[:], in0=guess[:], scalar=0.5, in1=half_quotient[:], op0=ALU.mult, op1=ALU.add
             )
+
 
         v_rows = {}
+        v_words = {}
+        v_mx = {}
 
         def stage_one(u, t):
-            a = u // 2
-            if t == 0:
-                v_rows[u] = work.tile([P, PACK, K_PASS], BF16, name="vrows", tag="vrows", align_bytes=64)
+            a = u // UNITS_PER_REGIME
             bank = take_bank()
             for g in range(PASSES):
                 nc.tensor.matmul_mx(
                     out=bank[:],
-                    lhsT=b_codes[a][:, t, 2 * P * g : 2 * P * (g + 1)].bitcast(FP4X4),
+                    lhsT=b_codes[a][:, t, FP4_BYTES * P * g : FP4_BYTES * P * (g + 1)].bitcast(FP4X4),
                     lhsT_scale=b_planes[a][:, t, P * g : P * (g + 1)],
-                    rhs=x_q[u, g][0][:].bitcast(FP8X4),
-                    rhs_scale=x_q[u, g][1][:],
+                    rhs=x_mx[u, g][0][:].bitcast(FP8X4),
+                    rhs_scale=x_mx[u, g][1][:],
                     start=(g == 0),
                     stop=(g == PASSES - 1),
                 )
-            c = PACK * a + t
-            nc.scalar.activation(out=v_rows[u][:, t, :], in_=bank[:], func=ACT.Square, scale=root[:, c : c + 1])
+            if t == 0:
+                v_rows[u] = work.tile([P, SLOTS, UNIT_ROWS], BF16, name="vrows", tag="vrows", align_bytes=64)
+            col = SLOTS * a + t
+            nc.scalar.activation(out=v_rows[u][:, t, :], in_=bank[:], func=ACT.Square, scale=root[:, col : col + 1])
 
-        v_q = {}
-
-        def new_v(u):
-            v_words = work.tile([P, K_PASS, PACK], BF16, name="vwords", tag="vwords", align_bytes=64)
-            codes = work.tile([P, K_PASS], U32, name="vc", tag="vc", align_bytes=64)
-            plane = work.tile([P, K_PASS], U8, name="vs", tag="vs", align_bytes=64)
-            v_q[u] = (v_words, codes, plane)
-
-        def interleave_v(u, j0, j1):
+        def interleave_v(u, c0, c1):
+            if c0 == 0:
+                v_words[u] = work.tile([P, UNIT_ROWS, SLOTS], BF16, name="vwords", tag="vwords", align_bytes=64)
             nc.vector.tensor_copy(
-                out=v_q[u][0][:, P * j0 : P * j1, :].rearrange("p (c i) t -> p c t i", i=4),
-                in_=v_rows[u][:, :, P * j0 : P * j1].rearrange("p t (c i) -> p c t i", i=4),
+                out=v_words[u][:, P * c0 : P * c1, :].rearrange("p (m i) t -> p m t i", i=4),
+                in_=v_rows[u][:, :, P * c0 : P * c1].rearrange("p t (m i) -> p m t i", i=4),
             )
 
-        def quantize_v(u, j0, j1):
-            v_words, codes, plane = v_q[u]
+        def quantize_v(u, c0, c1):
+            if c0 == 0:
+                codes = work.tile([P, UNIT_ROWS], U32, name="vcodes", tag="vcodes", align_bytes=64)
+                plane = work.tile([P, UNIT_ROWS], U8, name="vplane", tag="vplane", align_bytes=64)
+                v_mx[u] = (codes, plane)
             nc.vector.quantize_mx(
-                out=codes[:, P * j0 : P * j1].bitcast(FP8X4),
-                scales=plane[:, P * j0 : P * j1],
-                in_=v_words[:, P * j0 : P * j1, :].rearrange("p c t -> p (c t)"),
+                out=v_mx[u][0][:, P * c0 : P * c1].bitcast(FP8X4),
+                scales=v_mx[u][1][:, P * c0 : P * c1],
+                in_=v_words[u][:, P * c0 : P * c1, :].rearrange("p m t -> p (m t)"),
             )
+
 
         results = {}
 
-        def stage_two(u, j):
-            a = u // 2
-            v_words, codes, plane = v_q[u]
+        def stage_two(u, c, on_scalar):
+            a = u // UNITS_PER_REGIME
             bank = take_bank()
             nc.tensor.matmul_mx(
                 out=bank[:],
-                lhsT=codes[:, P * j : P * (j + 1)].bitcast(FP8X4),
-                lhsT_scale=plane[:, P * j : P * (j + 1)],
-                rhs=cw[:, 2 * R * a : 2 * R * (a + 1)].bitcast(FP4X4),
-                rhs_scale=cs[:, R * a : R * (a + 1)],
+                lhsT=v_mx[u][0][:, P * c : P * (c + 1)].bitcast(FP8X4),
+                lhsT_scale=v_mx[u][1][:, P * c : P * (c + 1)],
+                rhs=c_codes[:, FP4_BYTES * R * a : FP4_BYTES * R * (a + 1)].bitcast(FP4X4),
+                rhs_scale=c_planes[:, R * a : R * (a + 1)],
                 start=True,
                 stop=True,
             )
-            return bank
-
-        def finish(u, j, bank, on_scalar):
-            if j == 0:
-                results[u] = outs.tile([P, UNIT, R], F32, name="result", tag="result")
-            c = UNIT * u + j
+            if c == 0:
+                results[u] = outs.tile([P, TILES_PER_UNIT, R], F32, name="result", tag="result")
+            n = TILES_PER_UNIT * u + c
+            factor = inv_total[:, n : n + 1]
             if on_scalar:
-                nc.scalar.activation(out=results[u][:, j, :], in_=bank[:], func=ACT.Copy, scale=inv_tv[:, c : c + 1])
+                nc.scalar.activation(out=results[u][:, c, :], in_=bank[:], func=ACT.Copy, scale=factor)
             else:
                 nc.vector.tensor_scalar(
-                    out=results[u][:, j, :], in0=bank[:], scalar1=inv_tv[:, c : c + 1], scalar2=None, op0=ALU.mult
+                    out=results[u][:, c, :], in0=bank[:], scalar1=factor, scalar2=None, op0=ALU.mult
                 )
 
-        def store(u, j0, j1):
-            a, h = divmod(u, 2)
-            dst = out[a].rearrange("(p j) r -> p j r", j=ROWS)
-            nc.sync.dma_start(out=dst[:, UNIT * h + j0 : UNIT * h + j1, :], in_=results[u][:, j0:j1, :])
+        def store(u, c0, c1):
+            a, s = divmod(TILES_PER_UNIT * u, TILES_PER_REGIME)
+            dst = out[a].rearrange("(p s) r -> p s r", s=TILES_PER_REGIME)
+            nc.sync.dma_start(out=dst[:, s + c0 : s + c1, :], in_=results[u][:, c0:c1, :])
 
-        def pair(n, first, second):
-            transpose_pair(n, 0, first)
-            transpose_pair(n, 1, second)
+        make_root()
+        transpose_pair(0, ON_SCALAR)
+        sort_b_codes(0)
+        sort_b_scales(0)
+        for g in range(PASSES):
+            transpose_pass(2, g, ON_SCALAR)
+            quantize_x(0, g)
+        transpose_pair(4, ON_SCALAR)
+        sort_b_codes(1)
+        sort_b_codes(2)
+        sort_b_scales(1)
+        stage_one(0, 0)
+        stage_one(0, 1)
+        transpose_pair(6, ON_SCALAR)
+        for g in range(PASSES):
+            quantize_x(1, g)
+        stage_one(0, 2)
+        stage_one(0, 3)
+        transpose_pair(8, ON_SCALAR)
+        interleave_v(0, 0, TILES_PER_UNIT)
+        nc.vector.reciprocal(out=inv_total[:], in_=total[:].rearrange("p a s -> p (a s)"))
+        quantize_v(0, 0, TILES_PER_UNIT)
+        sort_b_scales(2)
 
-        polish_root()
-        pair(0, True, True)
-        sort_b(0, 0, 2)
-        transpose_pair(2, 0, True)
-        quantize_x(0, 0)
-        transpose_pair(2, 1, True)
-        quantize_x(0, 1)
-        sort_b(0, 2, 4)
-        pair(4, True, True)
-
-        last = UNITS - 1
-        for u in range(UNITS):
-            n = UNIT * u + AHEAD
-            early = u in (0, last - 1)
-            for t in range(PACK):
+        units_with_transposes = UNITS - 2
+        codes_step, scales_step = 2, 3
+        for u in range(1, units_with_transposes):
+            n = TILES_PER_UNIT * (u + 2)
+            for t in range(SLOTS):
                 stage_one(u, t)
-                if early and t == 1:
-                    pair(n, False, False)
-                    quantize_x(u + 1, 0)
-                    quantize_x(u + 1, 1)
-            if u == 0:
-                pair(n + 2, True, True)
-                nc.vector.reciprocal(out=inv_tv[:], in_=tv[:].rearrange("p a j -> p (a j)"))
-            elif n < TILES and not early:
-                pair(n, True, True)
-            new_v(u)
-            if u < last:
-                interleave_v(u, 0, UNIT)
-                if not early:
-                    quantize_x(u + 1, 0)
-                    quantize_x(u + 1, 1)
-                if u == 0:
-                    sort_b(1, 0, 2)
-                if u != last - 1:
-                    quantize_v(u, 0, UNIT)
-            a, h = divmod(u + 1, 2)
-            sorting = a + 1 < G
-            if u > 0:
-                for j in range(UNIT):
-                    finish(u - 1, j, stage_two(u - 1, j), j < 2 or u == last)
-                    if u == last - 1 and j == 2:
-                        quantize_v(u, 0, UNIT)
-                    if u == last:
-                        store(u - 1, j, j + 1)
-                    elif j % 2 == 1:
-                        store(u - 1, j - 1, j + 1)
-            if u > 0 and n + 2 < TILES:
-                pair(n + 2, True, sorting)
-            if sorting:
-                sort_b(a + 1, 2 * h, 2 * h + 2)
-        u = last
+                if u == 1 and t == 1:
+                    transpose_pair(n - 2, ON_VECTOR)
+                    for g in range(PASSES):
+                        quantize_x(2, g)
+            transpose_pair(n, ON_SCALAR)
+            interleave_v(u, 0, TILES_PER_UNIT)
+            stage_two(u - 1, 0, ON_SCALAR)
+            stage_two(u - 1, 1, ON_SCALAR)
+            store(u - 1, 0, 2)
+            stage_two(u - 1, 2, ON_VECTOR)
+            quantize_v(u, 0, TILES_PER_UNIT)
+            stage_two(u - 1, 3, ON_VECTOR)
+            store(u - 1, 2, 4)
+            transpose_pair(n + 2, u == codes_step)
+            for g in range(PASSES):
+                quantize_x(u + 2, g)
+            if u == codes_step:
+                sort_b_codes(G - 1)
+            if u == scales_step:
+                sort_b_scales(G - 1)
+
+        u = UNITS - 2
+        for t in range(SLOTS):
+            stage_one(u, t)
+        for c in range(TILES_PER_UNIT):
+            stage_two(u - 1, c, c == 1)
+            store(u - 1, c, c + 1)
+            if c == 0:
+                interleave_v(u, 0, TILES_PER_UNIT)
+            if c == 2:
+                quantize_v(u, 0, TILES_PER_UNIT)
+        u = UNITS - 1
+        for t in range(SLOTS):
+            stage_one(u, t)
+        for c in range(TILES_PER_UNIT):
+            stage_two(u - 1, c, ON_SCALAR)
+            store(u - 1, c, c + 1)
         interleave_v(u, 0, 1)
-        for j in range(UNIT):
-            if j + 1 < UNIT:
-                interleave_v(u, j + 1, j + 2)
-            quantize_v(u, j, j + 1)
-        for j in range(UNIT):
-            finish(u, j, stage_two(u, j), j % 2 == 1)
-            store(u, j, j + 1)
+        for c in range(TILES_PER_UNIT):
+            if c + 1 < TILES_PER_UNIT:
+                interleave_v(u, c + 1, c + 2)
+            quantize_v(u, c, c + 1)
+        for c in range(TILES_PER_UNIT):
+            stage_two(u, c, c % 2 == 1)
+            store(u, c, c + 1)

from contextlib import ExitStack

import concourse.mybir as mybir
from concourse.masks import make_identity

G, M, N, F, R = 4, 1024, 1024, 512, 512
FLOPS = 2 * G * M * (N * F + F * R)

F32 = mybir.dt.float32
BF16 = mybir.dt.bfloat16
I32 = mybir.dt.int32
U32 = mybir.dt.uint32
U8 = mybir.dt.uint8
FP8X4 = mybir.dt.float8_e4m3fn_x4
FP4X4 = mybir.dt.float4_e2m1fn_x4
ACT = mybir.ActivationFunctionType
ALU = mybir.AluOpType

P = 128
SLOTS = 4
K_PASS = P * SLOTS
PASSES = N // K_PASS
FP4_BYTES = 2
QUADRANT = 32
TILES_PER_REGIME = M // P
TILES_PER_UNIT = 4
UNIT_ROWS = TILES_PER_UNIT * P
UNITS_PER_REGIME = TILES_PER_REGIME // TILES_PER_UNIT
UNITS = G * UNITS_PER_REGIME
TILES = G * TILES_PER_REGIME
BANKS = 8
RESULT_BUFS = 6
ON_SCALAR, ON_VECTOR = True, False


def tile_svar_horizon_variance_contrasts_s14_kernel(
    tc, psi, b_words, b_scales, shock_var, c_words, c_scales, total_var, out
):
    nc = tc.nc
    with ExitStack() as ctx:
        keep = ctx.enter_context(tc.tile_pool(name="keep", bufs=1))
        work = ctx.enter_context(tc.tile_pool(name="work", bufs=2))
        outs = ctx.enter_context(tc.tile_pool(name="outs", bufs=RESULT_BUFS))
        psum = ctx.enter_context(tc.psum_pool(name="psum", bufs=1))
        ctx.enter_context(tc.manual_schedule())

        bank_uses = []

        def take_bank():
            name = "bank%d" % (len(bank_uses) % BANKS)
            bank = psum.tile([P, K_PASS], F32, name=name, tag=name)
            bank_uses.append(name)
            return bank

        ident = keep.tile([P, P], F32, align_bytes=64)
        make_identity(nc, ident[:])

        b_scale_first = keep.tile([P, PASSES * F], U8, align_bytes=64)
        b_scale_rest = keep.tile([P, (G - 1) * PASSES * F], U8, align_bytes=64)
        c_planes = keep.tile([P, G * R], U8, align_bytes=64)
        nc.vector.memset(b_scale_first[:].bitcast(I32), 0)
        nc.vector.memset(c_planes[:].bitcast(I32), 0)
        nc.vector.memset(b_scale_rest[:].bitcast(I32), 0)


        def load_scale_rows(planes, rows):
            for q in range(P // QUADRANT):
                nc.sync.dma_start(
                    out=planes[QUADRANT * q : QUADRANT * q + 4, :]
                    .bitcast(I32)
                    .rearrange("p (g w) -> p g w", g=rows.shape[0]),
                    in_=rows[:, 4 * q : 4 * q + 4, :].bitcast(I32).rearrange("g r w -> r g w"),
                )

        psi_words = {}

        def load_psi(n, count):
            a, s = divmod(n, TILES_PER_REGIME)
            rows = keep.tile([P, count, N], BF16, name="psi%d" % n, align_bytes=64)
            src = psi[a].rearrange("(p s) k -> p s k", s=TILES_PER_REGIME)
            nc.sync.dma_start(out=rows[:], in_=src[:, s : s + count, :])
            for i in range(0, count, 2):
                for g in range(PASSES):
                    psi_words[n + i, g] = rows[:, i : i + 2, g * K_PASS : (g + 1) * K_PASS].bitcast(F32)

        b_raw = {}

        def load_b_words(a):
            b_raw[a] = keep.tile([P, PASSES * FP4_BYTES * F], U8, name="braw%d" % a, align_bytes=64)
            nc.sync.dma_start(
                out=b_raw[a][:].bitcast(I32).rearrange("p (g w) -> p g w", g=PASSES),
                in_=b_words[PASSES * a : PASSES * (a + 1)].bitcast(I32).rearrange("g p w -> p g w"),
            )

        shock = keep.tile([P, G, SLOTS], BF16, align_bytes=64)
        total = keep.tile([P, G, TILES_PER_REGIME], BF16, align_bytes=64)
        c_codes = keep.tile([P, G * FP4_BYTES * R], U8, align_bytes=64)

        nc.scalar.dma_start(out=shock[:], in_=shock_var.rearrange("a (p t) -> p a t", t=SLOTS))
        load_psi(0, 2)
        load_b_words(0)
        load_scale_rows(b_scale_first, b_scales[0:PASSES])
        load_psi(2, 2)
        load_psi(4, 2)
        load_b_words(1)
        load_scale_rows(b_scale_rest, b_scales[PASSES:])
        load_psi(6, 2)
        load_b_words(2)
        load_psi(8, 2)
        load_psi(10, 2)
        nc.sync.dma_start(out=total[:], in_=total_var.rearrange("a (p s) -> p a s", s=TILES_PER_REGIME))
        nc.sync.dma_start(
            out=c_codes[:].bitcast(I32).rearrange("p (g w) -> p g w", g=G),
            in_=c_words.bitcast(I32).rearrange("g p w -> p g w"),
        )
        load_scale_rows(c_planes, c_scales)
        load_psi(12, TILES_PER_UNIT)
        load_b_words(3)
        for n in range(16, TILES, TILES_PER_UNIT):
            load_psi(n, TILES_PER_UNIT)


        b_codes = {}
        b_planes = {}

        def sort_b_codes(a):
            b_codes[a] = keep.tile([P, SLOTS, PASSES * FP4_BYTES * P], U8, name="bcodes%d" % a, align_bytes=64)
            nc.vector.tensor_copy(
                out=b_codes[a][:].rearrange("p t (m b) -> p t m b", b=FP4_BYTES),
                in_=b_raw[a][:].rearrange("p (m t b) -> p t m b", t=SLOTS, b=FP4_BYTES),
            )

        def sort_b_scales(a):
            width = PASSES * F
            raw = b_scale_first[:] if a == 0 else b_scale_rest[:, (a - 1) * width : a * width]
            b_planes[a] = keep.tile([P, SLOTS, PASSES * P], U8, name="bplane%d" % a, align_bytes=64)
            nc.vector.tensor_copy(out=b_planes[a][:], in_=raw.rearrange("p (m t) -> p t m", t=SLOTS))


        x_words = {}
        x_mx = {}

        def transpose_pass(n, g, on_scalar):
            u, c = divmod(n, TILES_PER_UNIT)
            if c == 0:
                name = "xwords%d" % g
                x_words[u, g] = work.tile([P, TILES_PER_UNIT, P, 2], F32, name=name, tag=name, align_bytes=64)
            bank = take_bank()
            for i in range(2):
                for odd in range(2):
                    col = (2 * i + odd) * P
                    nc.tensor.transpose(bank[:, col : col + P], psi_words[n, g][:, i, odd : 2 * P : 2], ident[:])
            dst = x_words[u, g][:, c : c + 2, :, :]
            src = bank[:].rearrange("p (i o r) -> p i r o", i=2, o=2)
            if on_scalar:
                nc.scalar.copy(out=dst, in_=src)
            else:
                nc.vector.tensor_copy(out=dst, in_=src)

        def transpose_pair(n, second_on_scalar):
            transpose_pass(n, 0, ON_SCALAR)
            transpose_pass(n, 1, second_on_scalar)

        def quantize_x(u, g):
            codes = work.tile([P, UNIT_ROWS], U32, name="xcodes%d" % g, tag="xcodes%d" % g, align_bytes=64)
            plane = work.tile([P, UNIT_ROWS], U8, name="xplane%d" % g, tag="xplane%d" % g, align_bytes=64)
            nc.vector.quantize_mx(
                out=codes[:].bitcast(FP8X4),
                scales=plane[:],
                in_=x_words[u, g][:].rearrange("p c r o -> p (c r o)").bitcast(BF16),
            )
            x_mx[u, g] = (codes, plane)


        root = keep.tile([P, G * SLOTS], F32)
        inv_total = keep.tile([P, TILES], F32)

        def make_root():
            shock_flat = shock[:].rearrange("p a t -> p (a t)")
            guess = keep.tile([P, G * SLOTS], F32)
            floored = keep.tile([P, G * SLOTS], F32)
            inv_guess = keep.tile([P, G * SLOTS], F32)
            half_quotient = keep.tile([P, G * SLOTS], F32)
            nc.scalar.activation(out=guess[:], in_=shock_flat, func=ACT.Sqrt)
            nc.vector.tensor_scalar(out=floored[:], in0=guess[:], scalar1=1e-30, scalar2=None, op0=ALU.max)
            nc.vector.reciprocal(out=inv_guess[:], in_=floored[:])
            nc.vector.scalar_tensor_tensor(
                out=half_quotient[:], in0=shock_flat, scalar=0.5, in1=inv_guess[:], op0=ALU.mult, op1=ALU.mult
            )
            nc.vector.scalar_tensor_tensor(
                out=root[:], in0=guess[:], scalar=0.5, in1=half_quotient[:], op0=ALU.mult, op1=ALU.add
            )


        v_rows = {}
        v_words = {}
        v_mx = {}

        def stage_one(u, t):
            a = u // UNITS_PER_REGIME
            bank = take_bank()
            for g in range(PASSES):
                nc.tensor.matmul_mx(
                    out=bank[:],
                    lhsT=b_codes[a][:, t, FP4_BYTES * P * g : FP4_BYTES * P * (g + 1)].bitcast(FP4X4),
                    lhsT_scale=b_planes[a][:, t, P * g : P * (g + 1)],
                    rhs=x_mx[u, g][0][:].bitcast(FP8X4),
                    rhs_scale=x_mx[u, g][1][:],
                    start=(g == 0),
                    stop=(g == PASSES - 1),
                )
            if t == 0:
                v_rows[u] = work.tile([P, SLOTS, UNIT_ROWS], BF16, name="vrows", tag="vrows", align_bytes=64)
            col = SLOTS * a + t
            nc.scalar.activation(out=v_rows[u][:, t, :], in_=bank[:], func=ACT.Square, scale=root[:, col : col + 1])

        def interleave_v(u, c0, c1):
            if c0 == 0:
                v_words[u] = work.tile([P, UNIT_ROWS, SLOTS], BF16, name="vwords", tag="vwords", align_bytes=64)
            nc.vector.tensor_copy(
                out=v_words[u][:, P * c0 : P * c1, :].rearrange("p (m i) t -> p m t i", i=4),
                in_=v_rows[u][:, :, P * c0 : P * c1].rearrange("p t (m i) -> p m t i", i=4),
            )

        def quantize_v(u, c0, c1):
            if c0 == 0:
                codes = work.tile([P, UNIT_ROWS], U32, name="vcodes", tag="vcodes", align_bytes=64)
                plane = work.tile([P, UNIT_ROWS], U8, name="vplane", tag="vplane", align_bytes=64)
                v_mx[u] = (codes, plane)
            nc.vector.quantize_mx(
                out=v_mx[u][0][:, P * c0 : P * c1].bitcast(FP8X4),
                scales=v_mx[u][1][:, P * c0 : P * c1],
                in_=v_words[u][:, P * c0 : P * c1, :].rearrange("p m t -> p (m t)"),
            )


        results = {}

        def stage_two(u, c, on_scalar):
            a = u // UNITS_PER_REGIME
            bank = take_bank()
            nc.tensor.matmul_mx(
                out=bank[:],
                lhsT=v_mx[u][0][:, P * c : P * (c + 1)].bitcast(FP8X4),
                lhsT_scale=v_mx[u][1][:, P * c : P * (c + 1)],
                rhs=c_codes[:, FP4_BYTES * R * a : FP4_BYTES * R * (a + 1)].bitcast(FP4X4),
                rhs_scale=c_planes[:, R * a : R * (a + 1)],
                start=True,
                stop=True,
            )
            if c == 0:
                results[u] = outs.tile([P, TILES_PER_UNIT, R], F32, name="result", tag="result")
            n = TILES_PER_UNIT * u + c
            factor = inv_total[:, n : n + 1]
            if on_scalar:
                nc.scalar.activation(out=results[u][:, c, :], in_=bank[:], func=ACT.Copy, scale=factor)
            else:
                nc.vector.tensor_scalar(
                    out=results[u][:, c, :], in0=bank[:], scalar1=factor, scalar2=None, op0=ALU.mult
                )

        def store(u, c0, c1):
            a, s = divmod(TILES_PER_UNIT * u, TILES_PER_REGIME)
            dst = out[a].rearrange("(p s) r -> p s r", s=TILES_PER_REGIME)
            nc.sync.dma_start(out=dst[:, s + c0 : s + c1, :], in_=results[u][:, c0:c1, :])

        make_root()
        transpose_pair(0, ON_SCALAR)
        sort_b_codes(0)
        sort_b_scales(0)
        for g in range(PASSES):
            transpose_pass(2, g, ON_SCALAR)
            quantize_x(0, g)
        transpose_pair(4, ON_SCALAR)
        sort_b_codes(1)
        sort_b_codes(2)
        sort_b_scales(1)
        stage_one(0, 0)
        stage_one(0, 1)
        transpose_pair(6, ON_SCALAR)
        for g in range(PASSES):
            quantize_x(1, g)
        stage_one(0, 2)
        stage_one(0, 3)
        transpose_pair(8, ON_SCALAR)
        interleave_v(0, 0, TILES_PER_UNIT)
        nc.vector.reciprocal(out=inv_total[:], in_=total[:].rearrange("p a s -> p (a s)"))
        quantize_v(0, 0, TILES_PER_UNIT)
        sort_b_scales(2)

        units_with_transposes = UNITS - 2
        codes_step, scales_step = 2, 3
        for u in range(1, units_with_transposes):
            n = TILES_PER_UNIT * (u + 2)
            for t in range(SLOTS):
                stage_one(u, t)
                if u == 1 and t == 1:
                    transpose_pair(n - 2, ON_VECTOR)
                    for g in range(PASSES):
                        quantize_x(2, g)
            transpose_pair(n, ON_SCALAR)
            interleave_v(u, 0, TILES_PER_UNIT)
            stage_two(u - 1, 0, ON_SCALAR)
            stage_two(u - 1, 1, ON_SCALAR)
            store(u - 1, 0, 2)
            stage_two(u - 1, 2, ON_VECTOR)
            quantize_v(u, 0, TILES_PER_UNIT)
            stage_two(u - 1, 3, ON_VECTOR)
            store(u - 1, 2, 4)
            transpose_pair(n + 2, u == codes_step)
            for g in range(PASSES):
                quantize_x(u + 2, g)
            if u == codes_step:
                sort_b_codes(G - 1)
            if u == scales_step:
                sort_b_scales(G - 1)

        u = UNITS - 2
        for t in range(SLOTS):
            stage_one(u, t)
        for c in range(TILES_PER_UNIT):
            stage_two(u - 1, c, c == 1)
            store(u - 1, c, c + 1)
            if c == 0:
                interleave_v(u, 0, TILES_PER_UNIT)
            if c == 2:
                quantize_v(u, 0, TILES_PER_UNIT)
        u = UNITS - 1
        for t in range(SLOTS):
            stage_one(u, t)
        for c in range(TILES_PER_UNIT):
            stage_two(u - 1, c, ON_SCALAR)
            store(u - 1, c, c + 1)
        interleave_v(u, 0, 1)
        for c in range(TILES_PER_UNIT):
            if c + 1 < TILES_PER_UNIT:
                interleave_v(u, c + 1, c + 2)
            quantize_v(u, c, c + 1)
        for c in range(TILES_PER_UNIT):
            stage_two(u, c, c % 2 == 1)
            store(u, c, c + 1)
